import numpy as np
import ml_dtypes


def mxq(x, axis, fmt="e4m3"):
    dtype, down = {"e4m3": (ml_dtypes.float8_e4m3fn, 7), "e5m2": (ml_dtypes.float8_e5m2, 14)}[fmt]
    v = np.moveaxis(np.asarray(x, np.float32).astype(ml_dtypes.bfloat16).astype(np.float64), axis, -1)
    blocks = v.reshape(v.shape[:-1] + (-1, 32))
    amax = np.abs(blocks).max(-1, keepdims=True)
    byte = np.maximum(np.where(amax > 0, np.frexp(amax)[1] - 1 + 127, 0) - down, 1)
    scale = np.exp2(byte - 127.0)
    codes = (blocks / scale).astype(np.float32).astype(dtype).astype(np.float64)
    return np.moveaxis((codes * scale).reshape(v.shape), -1, axis)


WIDE = False


def mx_kscale(k):
    if not WIDE:
        return np.ones(k)
    levels = np.array([10, -10, 5, -5, 0])
    if k % 512:
        return np.exp2(np.random.permutation(np.resize(levels, k // 32))).repeat(32)
    a = np.empty((k // 512, 16))
    for p in range(k // 512):
        a[p, :8] = np.random.permutation(np.resize(levels, 8))
        for g in range(8):
            far = levels[np.abs(levels - a[p, g]) >= 10]
            a[p, g + 8] = far[np.random.randint(len(far))]
    return np.exp2(a.ravel()).repeat(32)


BF16 = ml_dtypes.bfloat16


def bf(x):
    return np.asarray(x, np.float32).astype(BF16)


def f64(x):
    return np.asarray(x).astype(np.float64)


E2M1 = np.array([0.0, 0.5, 1.0, 1.5, 2.0, 3.0, 4.0, 6.0, -0.0, -0.5, -1.0, -1.5, -2.0, -3.0, -4.0, -6.0])


def pack_weight(w, fmt):
    k, n = w.shape
    w = f64(bf(w)).reshape(k // 32, 32, n)
    amax = np.abs(w).max(1)
    if fmt == "e4m3":
        byte = np.frexp(amax)[1] - 1 + 127 - 7
    else:
        mant, ex = np.frexp(amax / 6.0)
        byte = np.where(mant > 0.5, ex, ex - 1) + 127
    byte = np.clip(np.where(amax > 0, byte, 1), 1, 254)
    scaled = (w * np.exp2(127.0 - byte)[:, None, :]).reshape(k, n).astype(np.float32)
    by_word = np.ascontiguousarray(scaled.reshape(k // 512, 128, 4, n).transpose(0, 1, 3, 2))
    if fmt == "e4m3":
        words = by_word.astype(ml_dtypes.float8_e4m3fn).view(np.uint8)
    else:
        c = by_word.astype(ml_dtypes.float4_e2m1fn).view(np.uint8) & 0xF
        words = c[..., 0::2] | (c[..., 1::2] << 4)
    return np.ascontiguousarray(words), np.ascontiguousarray(byte.astype(np.uint8).reshape(k // 512, 16, n))


def unpack_weight(words, scales, fmt):
    g, p, n, _ = words.shape
    if fmt == "e4m3":
        vals = np.ascontiguousarray(words).view(ml_dtypes.float8_e4m3fn).astype(np.float64)
    else:
        nib = np.empty((g, p, n, 4), np.uint8)
        nib[..., 0::2] = words & 0xF
        nib[..., 1::2] = words >> 4
        vals = E2M1[nib]
    vals = vals * np.repeat(np.exp2(scales.astype(np.float64) - 127.0), 8, axis=1)[..., None]
    return vals.transpose(0, 1, 3, 2).reshape(g * 512, n)

E4M3FN = np.array([(-1.0 if i & 128 else 1.0) * ((1.0 + (i & 7) / 8.0) * 2.0 ** (((i >> 3) & 15) - 7) if i & 120 else (i & 7) * 2.0 ** -9) for i in range(256)])


def e4m3fn_bytes(y):
    return np.clip(np.asarray(y, np.float64), -448.0, 448.0).astype(np.float32).astype(ml_dtypes.float8_e4m3fn).view(np.uint8)


def e4m3fn_values(b):
    return E4M3FN[b]


N, D, K, V = 512, 512, 4, 2048


def log_sum_exp(x, axis):
    m = np.max(x, axis=axis, keepdims=True)
    return m + np.log(np.sum(np.exp(x - m), axis=axis, keepdims=True))


def log_normalize(x, axis):
    s = x - np.max(x, axis=axis, keepdims=True)
    return s - np.log(np.sum(np.exp(s), axis=axis, keepdims=True))


def draw0():
    s = mx_kscale(D)
    t = mx_kscale(D)
    h = bf(np.random.standard_normal((N, D)) * s)
    w = bf(np.random.standard_normal((K, D, D)) / np.sqrt(D) / s[None, :, None])
    g = bf((1.0 + 0.1 * np.random.standard_normal((K, D))) * t)
    u = bf(np.random.standard_normal((K, D)) * 2.0 / np.sqrt(D))
    emb = np.random.standard_normal((V, D)) * 3.0 / np.sqrt(D) / t
    words, scales = pack_weight(emb.T, "e4m3")
    return {"h": h,
            "w": w,
            "g": g,
            "u": u,
            "emb_words": words,
            "emb_scales": scales}


def core(h, w, g, u, emb_words, emb_scales):
    n, d = h.shape
    k = w.shape[0]
    vocab = emb_words.shape[2]
    c = mxq(f64(h), 1, "e4m3") @ mxq(f64(w), 1, "e4m3")
    t = np.tanh(c.transpose(1, 0, 2))
    a = t * f64(g)[None, :, :]
    aq = mxq(a.reshape(n * k, d), 1, "e4m3")
    l = (aq @ unpack_weight(emb_words, emb_scales, "e4m3")).reshape(n, k, vocab)
    z = np.sum(t * f64(u)[None, :, :], axis=-1)
    logpi = log_normalize(z, axis=-1)
    lp = log_normalize(l, axis=-1)
    joint = logpi[:, :, None] + lp
    mixed = np.squeeze(log_sum_exp(joint, axis=1), axis=1)
    return mixed + np.log(vocab)


def setup_inputs():
    drawn = draw0()
    full = np.asarray(drawn['w']).astype(np.float64)
    scale = (np.abs(full).reshape(4, 4, 128, 4, 128).max(axis=(2, 4)) / 448.0).astype(np.float32)
    given = {}
    for key, value in drawn.items():
        if key == 'w':
            given['w_bytes'] = e4m3fn_bytes(full / np.repeat(np.repeat(scale.astype(np.float64), 128, axis=1), 128, axis=2))
            given['w_scale'] = scale
        else:
            given[key] = value
    return given


def reference(h, w_bytes, w_scale, g, u, emb_words, emb_scales):
    return core(h, e4m3fn_values(w_bytes) * np.repeat(np.repeat(w_scale.astype(np.float64), 128, axis=1), 128, axis=2), g, u, emb_words, emb_scales)

@@ -1,0 +1,489 @@
+import math
+from contextlib import ExitStack
+
+import concourse.mybir as mybir
+from concourse.masks import make_identity
+
+F32 = mybir.dt.float32
+BF16 = mybir.dt.bfloat16
+I32 = mybir.dt.int32
+U32 = mybir.dt.uint32
+U8 = mybir.dt.uint8
+FP8 = mybir.dt.float8_e4m3fn
+FP8X4 = mybir.dt.float8_e4m3fn_x4
+ACT = mybir.ActivationFunctionType
+ALU = mybir.AluOpType
+AX = mybir.AxisListType
+
+N, D, K, V = 512, 512, 4, 2048
+P = 128
+PACK = 4
+TILES = N // P
+CHUNK = 512
+CHUNKS = V // CHUNK
+UNITS = TILES * K
+LN_SHIFT = 62
+PE_TERMS = {job: 2 for job in range(12)}
+LAG = 2
+
+FLOPS = 2 * N * D * K * D + 2 * N * K * D * V
+
+
+def tile_mixtureofsoftmaxeshead_d2p_kernel(tc, h, w_bytes, w_scale, g, u, emb_words, emb_scales, out):
+    nc = tc.nc
+    with ExitStack() as ctx:
+        keep = ctx.enter_context(tc.tile_pool(name="keep", bufs=1))
+        ring = ctx.enter_context(tc.tile_pool(name="ring", bufs=2))
+        big = ctx.enter_context(tc.tile_pool(name="big", bufs=12))
+        ps_logits = ctx.enter_context(tc.psum_pool(name="ps_logits", bufs=5))
+        ps_first = ctx.enter_context(tc.psum_pool(name="ps_first", bufs=1))
+        ps_gate = ctx.enter_context(tc.psum_pool(name="ps_gate", bufs=1))
+        ps_mix = ctx.enter_context(tc.psum_pool(name="ps_mix", bufs=1))
+
+        h_raw = [keep.tile([P, D], BF16, name="h_raw%d" % t, align_bytes=64) for t in range(TILES)]
+        w_raw = [keep.tile([P, PACK * D], U8, name="w_raw%d" % a, align_bytes=64) for a in range(K)]
+        e_codes = [keep.tile([P, CHUNK], U32, name="e_codes%d" % c, align_bytes=64) for c in range(CHUNKS)]
+        e_plane = keep.tile([P, V], U8, name="e_plane", align_bytes=64)
+        scale_all = keep.tile([P, 64], F32, name="scale_all")
+        scale_cols = keep.tile([P, 16], F32, name="scale_cols")
+        g_sb = keep.tile([P, K, PACK], BF16, name="g_sb")
+        u_sb = keep.tile([P, K, PACK], BF16, name="u_sb")
+        u_f32 = keep.tile([P, K, PACK], F32, name="u_f32")
+        ident = keep.tile([P, P], F32, name="ident", align_bytes=64)
+        floor = keep.tile([P, 1], F32, name="floor")
+        dummy = keep.tile([P, 1], F32, name="dummy")
+
+        def load_h(t):
+            nc.sync.dma_start(out=h_raw[t][:], in_=h[t * P : (t + 1) * P, :])
+
+        def load_w(a):
+            nc.sync.dma_start(out=w_raw[a][:], in_=w_bytes[a].rearrange("(p j) e -> p (j e)", j=PACK))
+
+        load_h(0)
+        nc.scalar.dma_start(out=scale_all[:], in_=w_scale.rearrange("a i j -> (a i j)").partition_broadcast(P))
+        load_w(0)
+        nc.scalar.dma_start(out=g_sb[:], in_=g.rearrange("k (p t) -> p k t", t=PACK))
+        nc.scalar.dma_start(out=u_sb[:], in_=u.rearrange("k (p t) -> p k t", t=PACK))
+        nc.vector.memset(e_plane[:].bitcast(I32), 0)
+        nc.vector.memset(floor[:], 2.0**-64)
+        make_identity(nc, ident[:])
+        load_w(1)
+        for q in range(4):
+            nc.sync.dma_start(
+                out=e_plane[32 * q : 32 * q + 4, :].bitcast(I32), in_=emb_scales[0][4 * q : 4 * q + 4, :].bitcast(I32)
+            )
+        words = emb_words[0].rearrange("p n t -> p (n t)")
+        for c in range(CHUNKS):
+            nc.sync.dma_start(
+                out=e_codes[c][:].bitcast(I32),
+                in_=words[:, c * CHUNK * PACK : (c + 1) * CHUNK * PACK].bitcast(I32),
+            )
+        load_w(2)
+        for t in range(1, TILES):
+            load_h(t)
+        load_w(3)
+
+        nc.scalar.activation(dummy[:], floor[:], ACT.Exp)
+
+        for i in range(4):
+            rows = slice(32 * i, 32 * i + 32)
+            nc.gpsimd.tensor_copy(
+                out=scale_cols[rows, :].rearrange("p (a j) -> p a j", j=4),
+                in_=scale_all[rows, :].rearrange("p (a i j) -> p a i j", i=4, j=4)[:, :, i, :],
+            )
+        nc.gpsimd.tensor_copy(out=u_f32[:], in_=u_sb[:])
+
+        h_codes = {}
+        h_plane = {}
+        w_codes = {}
+        w_plane = {}
+        w_wide = {}
+        w_inter = {}
+        h_turned = {}
+
+        def prep_h(t):
+            turned = ps_mix.tile([P, 2, P], F32, name="turned", tag="mix")
+            pairs = h_raw[t][:].bitcast(F32)
+            for half in range(2):
+                nc.tensor.transpose(turned[:, half, :], pairs[:, half : 2 * P : 2], ident[:])
+            h_turned[t] = turned
+
+        def pack_h(t):
+            turned = h_turned[t]
+            inter = ring.tile([P, P * PACK], BF16, name="h_inter", align_bytes=64)
+            (nc.vector.tensor_copy if t == 0 else nc.scalar.copy)(
+                out=inter[:].bitcast(F32).rearrange("p (r v) -> p r v", v=2), in_=turned[:].rearrange("p v r -> p r v")
+            )
+            h_codes[t] = keep.tile([P, P], U32, name="h_codes%d" % t, align_bytes=64)
+            h_plane[t] = keep.tile([P, P], U8, name="h_plane%d" % t, align_bytes=64)
+            nc.vector.quantize_mx(out=h_codes[t][:].bitcast(FP8X4), scales=h_plane[t][:], in_=inter[:])
+
+        def widen(a, engine_copy, lo, hi):
+            if a not in w_wide:
+                w_wide[a] = ring.tile([P, PACK * D], BF16, name="w_wide", align_bytes=64)
+            engine_copy(out=w_wide[a][:, lo:hi], in_=w_raw[a][:, lo:hi].bitcast(FP8))
+
+        def scale_w(a, js, on_scalar):
+            if a not in w_inter:
+                w_inter[a] = ring.tile([P, D * PACK], BF16, name="w_inter", align_bytes=64)
+            for j in js:
+                src = w_wide[a][:].rearrange("p (k j m t) -> p j t m k", k=PACK, j=4, t=PACK)[:, j]
+                dst = w_inter[a][:].rearrange("p (t j m k) -> p j t m k", t=PACK, j=4, k=PACK)[:, j]
+                col = scale_cols[:, 4 * a + j : 4 * a + j + 1]
+                if on_scalar:
+                    nc.scalar.activation(dst, src, ACT.Copy, scale=col)
+                else:
+                    nc.vector.tensor_scalar(dst, src, col, None, ALU.mult)
+
+        def quant_w(a):
+            w_codes[a] = keep.tile([P, D], U32, name="w_codes%d" % a, align_bytes=64)
+            w_plane[a] = keep.tile([P, D], U8, name="w_plane%d" % a, align_bytes=64)
+            nc.vector.quantize_mx(out=w_codes[a][:].bitcast(FP8X4), scales=w_plane[a][:], in_=w_inter[a][:])
+
+        t_sb = {}
+        a_inter = {}
+        a_codes = {}
+        a_plane = {}
+        logits = {}
+        expo = {}
+        z_ps = {}
+        sums = {}
+        gate = {}
+        weight = {}
+        mixed = {}
+
+        def first(i):
+            if i >= UNITS:
+                return
+            t, k = divmod(i, K)
+            c = ps_first.tile([P, PACK, P], F32, name="c")
+            for j in range(PACK):
+                cols = slice(j * P, (j + 1) * P)
+                nc.tensor.matmul_mx(
+                    out=c[:, j, :],
+                    lhsT=w_codes[k][:, cols].bitcast(FP8X4),
+                    lhsT_scale=w_plane[k][:, cols],
+                    rhs=h_codes[t][:].bitcast(FP8X4),
+                    rhs_scale=h_plane[t][:],
+                    start=True,
+                    stop=True,
+                )
+            t_sb[i] = ring.tile([P, P, PACK], F32, name="t_sb", bufs=3)
+            nc.scalar.activation(t_sb[i][:], c[:].rearrange("p t n -> p n t"), ACT.Tanh)
+
+        def gain(i, engine):
+            if i >= UNITS:
+                return
+            k = i % K
+            a_inter[i] = ring.tile([P, P, PACK], BF16, name="a_inter", bufs=3, align_bytes=64)
+            engine.tensor_tensor(
+                out=a_inter[i][:], in0=t_sb[i][:], in1=g_sb[:, k : k + 1, :].to_broadcast([P, P, PACK]), op=ALU.mult
+            )
+
+        def mixture_logit(i):
+            if i >= UNITS:
+                return
+            t, k = divmod(i, K)
+            if k == 0:
+                z_ps[t] = ps_gate.tile([P, K], F32, name="z_ps")
+            for j in range(PACK):
+                nc.tensor.matmul(
+                    z_ps[t][:, k : k + 1],
+                    lhsT=t_sb[i][:, :, j],
+                    rhs=u_f32[:, k, j : j + 1],
+                    start=(j == 0),
+                    stop=(j == PACK - 1),
+                )
+
+        def quant_a(i):
+            if i >= UNITS:
+                return
+            a_codes[i] = ring.tile([P, P], U32, name="a_codes", bufs=3, align_bytes=64)
+            a_plane[i] = ring.tile([P, P], U8, name="a_plane", bufs=3, align_bytes=64)
+            nc.vector.quantize_mx(
+                out=a_codes[i][:].bitcast(FP8X4), scales=a_plane[i][:], in_=a_inter[i][:].rearrange("p n t -> p (n t)")
+            )
+
+        neg_peak = {}
+
+        def second(i, c):
+            if i >= UNITS:
+                return
+            bank = ps_logits.tile([P, CHUNK], F32, name="bank")
+            nc.tensor.matmul_mx(
+                out=bank[:],
+                lhsT=a_codes[i][:].bitcast(FP8X4),
+                lhsT_scale=a_plane[i][:],
+                rhs=e_codes[c][:].bitcast(FP8X4),
+                rhs_scale=e_plane[:, c * CHUNK : (c + 1) * CHUNK],
+                start=True,
+                stop=True,
+            )
+            logits[i, c] = bank
+
+        def exps(i, c):
+            t, k = divmod(i, K)
+            if c == 0:
+                expo[i] = big.tile([P, V], F32, name="expo")
+                if k == 0:
+                    sums[t] = ring.tile([P, K, CHUNKS], F32, name="sums")
+                    neg_peak[t] = ring.tile([P, K, CHUNKS], F32, name="neg_peak")
+            neg = neg_peak[t][:, k, c : c + 1]
+            nc.vector.tensor_reduce(out=neg, in_=logits[i, c][:], axis=AX.X, op=ALU.max, negate=True)
+            nc.scalar.activation(
+                expo[i][:, c * CHUNK : (c + 1) * CHUNK],
+                logits[i, c][:],
+                ACT.Exp,
+                bias=neg,
+                accum_out=sums[t][:, k, c : c + 1],
+            )
+
+        def gate_exp(t):
+            neg = ring.tile([P, 1], F32, name="z_neg")
+            nc.vector.tensor_reduce(out=neg[:], in_=z_ps[t][:], axis=AX.X, op=ALU.max, negate=True)
+            ge = ring.tile([P, K], F32, name="gate_e")
+            gs = ring.tile([P, 1], F32, name="gate_s")
+            nc.scalar.activation(ge[:], z_ps[t][:], ACT.Exp, bias=neg[:, 0:1], accum_out=gs[:, 0:1])
+            gate[t] = (ge, gs)
+
+        def weight_steps(t, k0, k1):
+            kk = slice(k0, k1)
+            n = k1 - k0
+            full = [P, n, CHUNKS]
+            tiles = {}
+            for nm in ("low", "ssum", "rec", "scal"):
+                tiles[nm] = ring.tile([P, K], F32, name=nm)
+            for nm in ("dif", "fac", "part"):
+                tiles[nm] = ring.tile([P, K, CHUNKS], F32, name=nm)
+            if t not in weight:
+                weight[t] = ring.tile([P, K, CHUNKS], F32, name="weight")
+
+            def wide(nm):
+                return tiles[nm][:, kk].unsqueeze(2).to_broadcast(full)
+
+            def s1():
+                nc.vector.tensor_reduce(out=tiles["low"][:, kk], in_=neg_peak[t][:, kk, :], axis=AX.X, op=ALU.min)
+
+            def s2():
+                nc.vector.tensor_tensor(
+                    out=tiles["dif"][:, kk, :], in0=wide("low"), in1=neg_peak[t][:, kk, :], op=ALU.subtract
+                )
+                nc.scalar.activation(tiles["fac"][:, kk, :], tiles["dif"][:, kk, :], ACT.Exp)
+
+            def s3():
+                nc.vector.tensor_tensor(
+                    out=tiles["part"][:, kk, :], in0=sums[t][:, kk, :], in1=tiles["fac"][:, kk, :], op=ALU.mult
+                )
+
+            def s4():
+                nc.vector.tensor_reduce(out=tiles["ssum"][:, kk], in_=tiles["part"][:, kk, :], axis=AX.X, op=ALU.add)
+
+            def s5():
+                nc.vector.reciprocal(tiles["rec"][:, kk], tiles["ssum"][:, kk])
+
+            def s6():
+                nc.vector.tensor_tensor(out=tiles["scal"][:, kk], in0=tiles["rec"][:, kk], in1=gate[t][:, kk], op=ALU.mult)
+
+            def s7():
+                nc.vector.tensor_tensor(
+                    out=weight[t][:, kk, :], in0=tiles["fac"][:, kk, :], in1=wide("scal"), op=ALU.mult
+                )
+
+            return [s1, s2, None, None, s3, s4, s5, s6, s7]
+
+        def gate_steps(t):
+            neg = ring.tile([P, 1], F32, name="z_neg")
+            ge = ring.tile([P, K], F32, name="gate_e")
+            gs = ring.tile([P, 1], F32, name="gate_s")
+            gr = ring.tile([P, 1], F32, name="gate_r")
+            gate[t] = ring.tile([P, K], F32, name="gate_n")
+
+            def g1():
+                nc.vector.tensor_reduce(out=neg[:], in_=z_ps[t][:], axis=AX.X, op=ALU.max, negate=True)
+                nc.scalar.activation(ge[:], z_ps[t][:], ACT.Exp, bias=neg[:, 0:1], accum_out=gs[:, 0:1])
+
+            def g2():
+                nc.vector.reciprocal(gr[:], gs[:])
+
+            def g3():
+                nc.vector.tensor_scalar(gate[t][:], ge[:], gr[:, 0:1], 2.0**LN_SHIFT, ALU.mult, ALU.mult)
+
+            return [g1, None, None, g2, g3]
+
+        def mix_steps(job):
+            t, c = divmod(job, CHUNKS)
+            cols = slice(c * CHUNK, (c + 1) * CHUNK)
+            if c == 0:
+                mixed[t] = keep.tile([P, V], F32, name="mixed%d" % t)
+            n = PE_TERMS.get(job, 0)
+            acc = mixed[t][:, cols]
+
+            def column(k):
+                return weight[t][:, k, c : c + 1]
+
+            diags = []
+            for k in range(n):
+                d = ring.tile([P, P], F32, name="diag", bufs=6)
+                nc.gpsimd.tensor_scalar(d[:], ident[:], column(k), 0.0, ALU.mult, ALU.add)
+                diags.append(d)
+
+            def term(k):
+                def run():
+                    if k == 0:
+                        banks[job] = ps_mix.tile([P, CHUNK], F32, name="mix_bank", tag="mix")
+                    nc.tensor.matmul(
+                        banks[job][:], lhsT=diags[k][:], rhs=expo[t * K + k][:, cols], start=(k == 0), stop=(k == n - 1)
+                    )
+
+                return run
+
+            def scaled():
+                nc.vector.tensor_scalar(acc, expo[t * K][:, cols], column(0), None, ALU.mult)
+
+            def add(k):
+                def run():
+                    nc.vector.scalar_tensor_tensor(
+                        out=acc,
+                        in0=expo[t * K + k][:, cols],
+                        scalar=column(k),
+                        in1=(banks[job][:] if k == n else acc),
+                        op0=ALU.mult,
+                        op1=ALU.add,
+                    )
+
+                return run
+
+            if n == 0:
+                return [], [scaled] + [add(k) for k in range(1, K)]
+            return [term(k) for k in range(n)], [add(k) for k in range(n, K)]
+
+        banks = {}
+
+        def log(t, lo, hi):
+            nc.scalar.activation(mixed[t][:, lo:hi], mixed[t][:, lo:hi], ACT.Ln, bias=floor[:, 0:1])
+
+        def finish(t, lo, hi):
+            part = mixed[t][:, lo:hi]
+            nc.vector.tensor_scalar(part, part, math.log(V) - LN_SHIFT * math.log(2.0), None, ALU.add)
+            nc.sync.dma_start(out=out[t * P : (t + 1) * P, lo:hi], in_=part)
+
+        W = PACK * D
+        SPLIT = W // 4
+        ALL = [0, 1, 2, 3]
+        prep_h(0)
+        pack_h(0)
+        widen(0, nc.scalar.copy, 0, SPLIT)
+        widen(0, nc.vector.tensor_copy, SPLIT, W)
+        scale_w(0, ALL[3:], True)
+        scale_w(0, ALL[:3], False)
+        quant_w(0)
+        widen(1, nc.scalar.copy, 0, W)
+        first(0)
+        scale_w(1, ALL, False)
+        gain(0, nc.vector)
+        quant_a(0)
+        for c in range(CHUNKS):
+            second(0, c)
+        quant_w(1)
+        first(1)
+        gain(1, nc.gpsimd)
+        mixture_logit(0)
+        widen(2, nc.scalar.copy, 0, W)
+        prep_h(1)
+        pack_h(1)
+
+        small = []
+        large = []
+        terms = []
+        fresh = []
+        coming = ([], [])
+
+        def one(queue):
+            step = queue.pop(0) if queue else None
+            if step:
+                step()
+
+        for i in range(UNITS):
+            t, k = divmod(i, K)
+            if k == 3:
+                small += gate_steps(t)
+            if k == 0 and t > 0:
+                small += weight_steps(t - 1, 0, K)
+            if i == UNITS - 1:
+                small += weight_steps(t, 0, K - 1)
+            job = i - K - LAG
+            large += fresh
+            fresh = coming[1]
+            terms += coming[0]
+            coming = mix_steps(job) if job >= 0 else ([], [])
+            for c in range(CHUNKS):
+                exps(i, c)
+                one(small)
+                if c == 0 and i <= 2:
+                    quant_a(i + 1)
+                if c == 2 and i >= 2:
+                    quant_a(i + 2)
+                if c == 1 and i == 0:
+                    scale_w(2, ALL, False)
+                    quant_w(2)
+                if c == 1 and i == 1:
+                    scale_w(3, ALL, False)
+                    quant_w(3)
+                second(i + 1, c)
+                if c % 2:
+                    one(large)
+                    one(small)
+                if c == 0 and i >= 2:
+                    first(i + 3)
+                    gain(i + 3, nc.gpsimd)
+                if c == 2:
+                    mixture_logit(i + 1 if i < 2 else i + 2)
+                if c in (1, 3):
+                    one(terms)
+            if i == 0:
+                first(2)
+                gain(2, nc.gpsimd)
+                widen(3, nc.scalar.copy, 0, W)
+                prep_h(2)
+                pack_h(2)
+            if i == 1:
+                first(3)
+                gain(3, nc.gpsimd)
+                first(4)
+                gain(4, nc.gpsimd)
+                prep_h(3)
+                pack_h(3)
+            if i == 2:
+                mixture_logit(3)
+
+        last = TILES - 1
+        while small:
+            one(small)
+        jobs = [(terms + coming[0], coming[1])] + [mix_steps(job) for job in range(UNITS - K - LAG, UNITS - K)]
+        large += fresh
+        for mm, adds in jobs:
+            for s in large:
+                s()
+            large = adds
+            for s in mm:
+                s()
+        for s in large:
+            s()
+        fins = []
+        for c in range(CHUNKS):
+            mm, adds = mix_steps(last * K + c)
+            for s in mm + adds[:-1]:
+                s()
+            fins.append(adds[-1])
+        for t in range(last):
+            log(t, 0, V)
+        for s in weight_steps(last, K - 1, K):
+            if s:
+                s()
+        for s in fins:
+            s()
+        for t in range(last):
+            finish(t, 0, V)
+        for c in range(CHUNKS):
+            log(last, c * CHUNK, (c + 1) * CHUNK)
+            finish(last, c * CHUNK, (c + 1) * CHUNK)

@@ -23,8 +23,13 @@ CHUNK = 512
 CHUNKS = V // CHUNK
 UNITS = TILES * K
 LN_SHIFT = 62
-PE_TERMS = {job: 2 for job in range(12)}
+PE_TERMS = {job: 3 for job in range(10)}
 LAG = 2
+
+
+def GAIN(nc):
+    return nc.vector
+
 
 FLOPS = 2 * N * D * K * D + 2 * N * K * D * V
 
@@ -168,8 +173,8 @@ def tile_mixtureofsoftmaxeshead_d2p_kernel(tc, h, w_bytes, w_scale, g, u, emb_wo
                     start=True,
                     stop=True,
                 )
-            t_sb[i] = ring.tile([P, P, PACK], F32, name="t_sb", bufs=3)
-            nc.scalar.activation(t_sb[i][:], c[:].rearrange("p t n -> p n t"), ACT.Tanh)
+            t_sb[i] = ring.tile([P, PACK, P], F32, name="t_sb", bufs=3)
+            nc.scalar.activation(t_sb[i][:], c[:], ACT.Tanh)
 
         def gain(i, engine):
             if i >= UNITS:
@@ -177,7 +182,7 @@ def tile_mixtureofsoftmaxeshead_d2p_kernel(tc, h, w_bytes, w_scale, g, u, emb_wo
             k = i % K
             a_inter[i] = ring.tile([P, P, PACK], BF16, name="a_inter", bufs=3, align_bytes=64)
             engine.tensor_tensor(
-                out=a_inter[i][:], in0=t_sb[i][:], in1=g_sb[:, k : k + 1, :].to_broadcast([P, P, PACK]), op=ALU.mult
+                out=a_inter[i][:], in0=t_sb[i][:].rearrange("p t n -> p n t"), in1=g_sb[:, k : k + 1, :].to_broadcast([P, P, PACK]), op=ALU.mult
             )
 
         def mixture_logit(i):
@@ -189,7 +194,7 @@ def tile_mixtureofsoftmaxeshead_d2p_kernel(tc, h, w_bytes, w_scale, g, u, emb_wo
             for j in range(PACK):
                 nc.tensor.matmul(
                     z_ps[t][:, k : k + 1],
-                    lhsT=t_sb[i][:, :, j],
+                    lhsT=t_sb[i][:, j, :],
                     rhs=u_f32[:, k, j : j + 1],
                     start=(j == 0),
                     stop=(j == PACK - 1),
@@ -282,7 +287,14 @@ def tile_mixtureofsoftmaxeshead_d2p_kernel(tc, h, w_bytes, w_scale, g, u, emb_wo
                 nc.vector.reciprocal(tiles["rec"][:, kk], tiles["ssum"][:, kk])
 
             def s6():
-                nc.vector.tensor_tensor(out=tiles["scal"][:, kk], in0=tiles["rec"][:, kk], in1=gate[t][:, kk], op=ALU.mult)
+                nc.vector.scalar_tensor_tensor(
+                    out=tiles["scal"][:, kk],
+                    in0=tiles["rec"][:, kk],
+                    scalar=2.0**LN_SHIFT,
+                    in1=gate[t][:, kk],
+                    op0=ALU.mult,
+                    op1=ALU.mult,
+                )
 
             def s7():
                 nc.vector.tensor_tensor(
@@ -295,20 +307,17 @@ def tile_mixtureofsoftmaxeshead_d2p_kernel(tc, h, w_bytes, w_scale, g, u, emb_wo
             neg = ring.tile([P, 1], F32, name="z_neg")
             ge = ring.tile([P, K], F32, name="gate_e")
             gs = ring.tile([P, 1], F32, name="gate_s")
-            gr = ring.tile([P, 1], F32, name="gate_r")
-            gate[t] = ring.tile([P, K], F32, name="gate_n")
+            gate[t] = ge
+            inv_gates[t] = keep.tile([P, 1], F32, name="inv_gates%d" % t)
 
             def g1():
                 nc.vector.tensor_reduce(out=neg[:], in_=z_ps[t][:], axis=AX.X, op=ALU.max, negate=True)
                 nc.scalar.activation(ge[:], z_ps[t][:], ACT.Exp, bias=neg[:, 0:1], accum_out=gs[:, 0:1])
 
             def g2():
-                nc.vector.reciprocal(gr[:], gs[:])
+                nc.vector.reciprocal(inv_gates[t][:], gs[:])
 
-            def g3():
-                nc.vector.tensor_scalar(gate[t][:], ge[:], gr[:, 0:1], 2.0**LN_SHIFT, ALU.mult, ALU.mult)
-
-            return [g1, None, None, g2, g3]
+            return [g1, None, None, g2]
 
         def mix_steps(job):
             t, c = divmod(job, CHUNKS)
@@ -338,7 +347,7 @@ def tile_mixtureofsoftmaxeshead_d2p_kernel(tc, h, w_bytes, w_scale, g, u, emb_wo
                 return run
 
             def scaled():
-                nc.vector.tensor_scalar(acc, expo[t * K][:, cols], column(0), None, ALU.mult)
+                nc.scalar.activation(acc, expo[t * K][:, cols], ACT.Copy, scale=column(0))
 
             def add(k):
                 def run():
@@ -358,9 +367,10 @@ def tile_mixtureofsoftmaxeshead_d2p_kernel(tc, h, w_bytes, w_scale, g, u, emb_wo
             return [term(k) for k in range(n)], [add(k) for k in range(n, K)]
 
         banks = {}
+        inv_gates = {}
 
         def log(t, lo, hi):
-            nc.scalar.activation(mixed[t][:, lo:hi], mixed[t][:, lo:hi], ACT.Ln, bias=floor[:, 0:1])
+            nc.scalar.activation(mixed[t][:, lo:hi], mixed[t][:, lo:hi], ACT.Ln, bias=floor[:, 0:1], scale=inv_gates[t][:, 0:1])
 
         def finish(t, lo, hi):
             part = mixed[t][:, lo:hi]
@@ -386,7 +396,7 @@ def tile_mixtureofsoftmaxeshead_d2p_kernel(tc, h, w_bytes, w_scale, g, u, emb_wo
             second(0, c)
         quant_w(1)
         first(1)
-        gain(1, nc.gpsimd)
+        gain(1, GAIN(nc))
         mixture_logit(0)
         widen(2, nc.scalar.copy, 0, W)
         prep_h(1)
@@ -427,7 +437,7 @@ def tile_mixtureofsoftmaxeshead_d2p_kernel(tc, h, w_bytes, w_scale, g, u, emb_wo
                     scale_w(2, ALL, False)
                     quant_w(2)
                 if c == 1 and i == 1:
-                    scale_w(3, ALL, False)
+                    scale_w(3, ALL, True)
                     quant_w(3)
                 second(i + 1, c)
                 if c % 2:
@@ -435,22 +445,22 @@ def tile_mixtureofsoftmaxeshead_d2p_kernel(tc, h, w_bytes, w_scale, g, u, emb_wo
                     one(small)
                 if c == 0 and i >= 2:
                     first(i + 3)
-                    gain(i + 3, nc.gpsimd)
+                    gain(i + 3, GAIN(nc))
                 if c == 2:
                     mixture_logit(i + 1 if i < 2 else i + 2)
-                if c in (1, 3):
+                if c >= 1:
                     one(terms)
             if i == 0:
                 first(2)
-                gain(2, nc.gpsimd)
+                gain(2, GAIN(nc))
                 widen(3, nc.scalar.copy, 0, W)
                 prep_h(2)
                 pack_h(2)
             if i == 1:
                 first(3)
-                gain(3, nc.gpsimd)
+                gain(3, GAIN(nc))
                 first(4)
-                gain(4, nc.gpsimd)
+                gain(4, GAIN(nc))
                 prep_h(3)
                 pack_h(3)
             if i == 2:

import math
from contextlib import ExitStack

import concourse.mybir as mybir
from concourse.masks import make_identity

F32 = mybir.dt.float32
BF16 = mybir.dt.bfloat16
I32 = mybir.dt.int32
U32 = mybir.dt.uint32
U8 = mybir.dt.uint8
FP8 = mybir.dt.float8_e4m3fn
FP8X4 = mybir.dt.float8_e4m3fn_x4
ACT = mybir.ActivationFunctionType
ALU = mybir.AluOpType
AX = mybir.AxisListType

N, D, K, V = 512, 512, 4, 2048
P = 128
PACK = 4
TILES = N // P
CHUNK = 512
CHUNKS = V // CHUNK
UNITS = TILES * K
LN_SHIFT = 62
PE_TERMS = {job: 3 for job in range(10)}
LAG = 2


def GAIN(nc):
    return nc.vector


FLOPS = 2 * N * D * K * D + 2 * N * K * D * V


def tile_mixtureofsoftmaxeshead_d2p_kernel(tc, h, w_bytes, w_scale, g, u, emb_words, emb_scales, out):
    nc = tc.nc
    with ExitStack() as ctx:
        keep = ctx.enter_context(tc.tile_pool(name="keep", bufs=1))
        ring = ctx.enter_context(tc.tile_pool(name="ring", bufs=2))
        big = ctx.enter_context(tc.tile_pool(name="big", bufs=12))
        ps_logits = ctx.enter_context(tc.psum_pool(name="ps_logits", bufs=5))
        ps_first = ctx.enter_context(tc.psum_pool(name="ps_first", bufs=1))
        ps_gate = ctx.enter_context(tc.psum_pool(name="ps_gate", bufs=1))
        ps_mix = ctx.enter_context(tc.psum_pool(name="ps_mix", bufs=1))

        h_raw = [keep.tile([P, D], BF16, name="h_raw%d" % t, align_bytes=64) for t in range(TILES)]
        w_raw = [keep.tile([P, PACK * D], U8, name="w_raw%d" % a, align_bytes=64) for a in range(K)]
        e_codes = [keep.tile([P, CHUNK], U32, name="e_codes%d" % c, align_bytes=64) for c in range(CHUNKS)]
        e_plane = keep.tile([P, V], U8, name="e_plane", align_bytes=64)
        scale_all = keep.tile([P, 64], F32, name="scale_all")
        scale_cols = keep.tile([P, 16], F32, name="scale_cols")
        g_sb = keep.tile([P, K, PACK], BF16, name="g_sb")
        u_sb = keep.tile([P, K, PACK], BF16, name="u_sb")
        u_f32 = keep.tile([P, K, PACK], F32, name="u_f32")
        ident = keep.tile([P, P], F32, name="ident", align_bytes=64)
        floor = keep.tile([P, 1], F32, name="floor")
        dummy = keep.tile([P, 1], F32, name="dummy")

        def load_h(t):
            nc.sync.dma_start(out=h_raw[t][:], in_=h[t * P : (t + 1) * P, :])

        def load_w(a):
            nc.sync.dma_start(out=w_raw[a][:], in_=w_bytes[a].rearrange("(p j) e -> p (j e)", j=PACK))

        load_h(0)
        nc.scalar.dma_start(out=scale_all[:], in_=w_scale.rearrange("a i j -> (a i j)").partition_broadcast(P))
        load_w(0)
        nc.scalar.dma_start(out=g_sb[:], in_=g.rearrange("k (p t) -> p k t", t=PACK))
        nc.scalar.dma_start(out=u_sb[:], in_=u.rearrange("k (p t) -> p k t", t=PACK))
        nc.vector.memset(e_plane[:].bitcast(I32), 0)
        nc.vector.memset(floor[:], 2.0**-64)
        make_identity(nc, ident[:])
        load_w(1)
        for q in range(4):
            nc.sync.dma_start(
                out=e_plane[32 * q : 32 * q + 4, :].bitcast(I32), in_=emb_scales[0][4 * q : 4 * q + 4, :].bitcast(I32)
            )
        words = emb_words[0].rearrange("p n t -> p (n t)")
        for c in range(CHUNKS):
            nc.sync.dma_start(
                out=e_codes[c][:].bitcast(I32),
                in_=words[:, c * CHUNK * PACK : (c + 1) * CHUNK * PACK].bitcast(I32),
            )
        load_w(2)
        for t in range(1, TILES):
            load_h(t)
        load_w(3)

        nc.scalar.activation(dummy[:], floor[:], ACT.Exp)

        for i in range(4):
            rows = slice(32 * i, 32 * i + 32)
            nc.gpsimd.tensor_copy(
                out=scale_cols[rows, :].rearrange("p (a j) -> p a j", j=4),
                in_=scale_all[rows, :].rearrange("p (a i j) -> p a i j", i=4, j=4)[:, :, i, :],
            )
        nc.gpsimd.tensor_copy(out=u_f32[:], in_=u_sb[:])

        h_codes = {}
        h_plane = {}
        w_codes = {}
        w_plane = {}
        w_wide = {}
        w_inter = {}
        h_turned = {}

        def prep_h(t):
            turned = ps_mix.tile([P, 2, P], F32, name="turned", tag="mix")
            pairs = h_raw[t][:].bitcast(F32)
            for half in range(2):
                nc.tensor.transpose(turned[:, half, :], pairs[:, half : 2 * P : 2], ident[:])
            h_turned[t] = turned

        def pack_h(t):
            turned = h_turned[t]
            inter = ring.tile([P, P * PACK], BF16, name="h_inter", align_bytes=64)
            (nc.vector.tensor_copy if t == 0 else nc.scalar.copy)(
                out=inter[:].bitcast(F32).rearrange("p (r v) -> p r v", v=2), in_=turned[:].rearrange("p v r -> p r v")
            )
            h_codes[t] = keep.tile([P, P], U32, name="h_codes%d" % t, align_bytes=64)
            h_plane[t] = keep.tile([P, P], U8, name="h_plane%d" % t, align_bytes=64)
            nc.vector.quantize_mx(out=h_codes[t][:].bitcast(FP8X4), scales=h_plane[t][:], in_=inter[:])

        def widen(a, engine_copy, lo, hi):
            if a not in w_wide:
                w_wide[a] = ring.tile([P, PACK * D], BF16, name="w_wide", align_bytes=64)
            engine_copy(out=w_wide[a][:, lo:hi], in_=w_raw[a][:, lo:hi].bitcast(FP8))

        def scale_w(a, js, on_scalar):
            if a not in w_inter:
                w_inter[a] = ring.tile([P, D * PACK], BF16, name="w_inter", align_bytes=64)
            for j in js:
                src = w_wide[a][:].rearrange("p (k j m t) -> p j t m k", k=PACK, j=4, t=PACK)[:, j]
                dst = w_inter[a][:].rearrange("p (t j m k) -> p j t m k", t=PACK, j=4, k=PACK)[:, j]
                col = scale_cols[:, 4 * a + j : 4 * a + j + 1]
                if on_scalar:
                    nc.scalar.activation(dst, src, ACT.Copy, scale=col)
                else:
                    nc.vector.tensor_scalar(dst, src, col, None, ALU.mult)

        def quant_w(a):
            w_codes[a] = keep.tile([P, D], U32, name="w_codes%d" % a, align_bytes=64)
            w_plane[a] = keep.tile([P, D], U8, name="w_plane%d" % a, align_bytes=64)
            nc.vector.quantize_mx(out=w_codes[a][:].bitcast(FP8X4), scales=w_plane[a][:], in_=w_inter[a][:])

        t_sb = {}
        a_inter = {}
        a_codes = {}
        a_plane = {}
        logits = {}
        expo = {}
        z_ps = {}
        sums = {}
        gate = {}
        weight = {}
        mixed = {}

        def first(i):
            if i >= UNITS:
                return
            t, k = divmod(i, K)
            c = ps_first.tile([P, PACK, P], F32, name="c")
            for j in range(PACK):
                cols = slice(j * P, (j + 1) * P)
                nc.tensor.matmul_mx(
                    out=c[:, j, :],
                    lhsT=w_codes[k][:, cols].bitcast(FP8X4),
                    lhsT_scale=w_plane[k][:, cols],
                    rhs=h_codes[t][:].bitcast(FP8X4),
                    rhs_scale=h_plane[t][:],
                    start=True,
                    stop=True,
                )
            t_sb[i] = ring.tile([P, PACK, P], F32, name="t_sb", bufs=3)
            nc.scalar.activation(t_sb[i][:], c[:], ACT.Tanh)

        def gain(i, engine):
            if i >= UNITS:
                return
            k = i % K
            a_inter[i] = ring.tile([P, P, PACK], BF16, name="a_inter", bufs=3, align_bytes=64)
            engine.tensor_tensor(
                out=a_inter[i][:], in0=t_sb[i][:].rearrange("p t n -> p n t"), in1=g_sb[:, k : k + 1, :].to_broadcast([P, P, PACK]), op=ALU.mult
            )

        def mixture_logit(i):
            if i >= UNITS:
                return
            t, k = divmod(i, K)
            if k == 0:
                z_ps[t] = ps_gate.tile([P, K], F32, name="z_ps")
            for j in range(PACK):
                nc.tensor.matmul(
                    z_ps[t][:, k : k + 1],
                    lhsT=t_sb[i][:, j, :],
                    rhs=u_f32[:, k, j : j + 1],
                    start=(j == 0),
                    stop=(j == PACK - 1),
                )

        def quant_a(i):
            if i >= UNITS:
                return
            a_codes[i] = ring.tile([P, P], U32, name="a_codes", bufs=3, align_bytes=64)
            a_plane[i] = ring.tile([P, P], U8, name="a_plane", bufs=3, align_bytes=64)
            nc.vector.quantize_mx(
                out=a_codes[i][:].bitcast(FP8X4), scales=a_plane[i][:], in_=a_inter[i][:].rearrange("p n t -> p (n t)")
            )

        neg_peak = {}

        def second(i, c):
            if i >= UNITS:
                return
            bank = ps_logits.tile([P, CHUNK], F32, name="bank")
            nc.tensor.matmul_mx(
                out=bank[:],
                lhsT=a_codes[i][:].bitcast(FP8X4),
                lhsT_scale=a_plane[i][:],
                rhs=e_codes[c][:].bitcast(FP8X4),
                rhs_scale=e_plane[:, c * CHUNK : (c + 1) * CHUNK],
                start=True,
                stop=True,
            )
            logits[i, c] = bank

        def exps(i, c):
            t, k = divmod(i, K)
            if c == 0:
                expo[i] = big.tile([P, V], F32, name="expo")
                if k == 0:
                    sums[t] = ring.tile([P, K, CHUNKS], F32, name="sums")
                    neg_peak[t] = ring.tile([P, K, CHUNKS], F32, name="neg_peak")
            neg = neg_peak[t][:, k, c : c + 1]
            nc.vector.tensor_reduce(out=neg, in_=logits[i, c][:], axis=AX.X, op=ALU.max, negate=True)
            nc.scalar.activation(
                expo[i][:, c * CHUNK : (c + 1) * CHUNK],
                logits[i, c][:],
                ACT.Exp,
                bias=neg,
                accum_out=sums[t][:, k, c : c + 1],
            )

        def gate_exp(t):
            neg = ring.tile([P, 1], F32, name="z_neg")
            nc.vector.tensor_reduce(out=neg[:], in_=z_ps[t][:], axis=AX.X, op=ALU.max, negate=True)
            ge = ring.tile([P, K], F32, name="gate_e")
            gs = ring.tile([P, 1], F32, name="gate_s")
            nc.scalar.activation(ge[:], z_ps[t][:], ACT.Exp, bias=neg[:, 0:1], accum_out=gs[:, 0:1])
            gate[t] = (ge, gs)

        def weight_steps(t, k0, k1):
            kk = slice(k0, k1)
            n = k1 - k0
            full = [P, n, CHUNKS]
            tiles = {}
            for nm in ("low", "ssum", "rec", "scal"):
                tiles[nm] = ring.tile([P, K], F32, name=nm)
            for nm in ("dif", "fac", "part"):
                tiles[nm] = ring.tile([P, K, CHUNKS], F32, name=nm)
            if t not in weight:
                weight[t] = ring.tile([P, K, CHUNKS], F32, name="weight")

            def wide(nm):
                return tiles[nm][:, kk].unsqueeze(2).to_broadcast(full)

            def s1():
                nc.vector.tensor_reduce(out=tiles["low"][:, kk], in_=neg_peak[t][:, kk, :], axis=AX.X, op=ALU.min)

            def s2():
                nc.vector.tensor_tensor(
                    out=tiles["dif"][:, kk, :], in0=wide("low"), in1=neg_peak[t][:, kk, :], op=ALU.subtract
                )
                nc.scalar.activation(tiles["fac"][:, kk, :], tiles["dif"][:, kk, :], ACT.Exp)

            def s3():
                nc.vector.tensor_tensor(
                    out=tiles["part"][:, kk, :], in0=sums[t][:, kk, :], in1=tiles["fac"][:, kk, :], op=ALU.mult
                )

            def s4():
                nc.vector.tensor_reduce(out=tiles["ssum"][:, kk], in_=tiles["part"][:, kk, :], axis=AX.X, op=ALU.add)

            def s5():
                nc.vector.reciprocal(tiles["rec"][:, kk], tiles["ssum"][:, kk])

            def s6():
                nc.vector.scalar_tensor_tensor(
                    out=tiles["scal"][:, kk],
                    in0=tiles["rec"][:, kk],
                    scalar=2.0**LN_SHIFT,
                    in1=gate[t][:, kk],
                    op0=ALU.mult,
                    op1=ALU.mult,
                )

            def s7():
                nc.vector.tensor_tensor(
                    out=weight[t][:, kk, :], in0=tiles["fac"][:, kk, :], in1=wide("scal"), op=ALU.mult
                )

            return [s1, s2, None, None, s3, s4, s5, s6, s7]

        def gate_steps(t):
            neg = ring.tile([P, 1], F32, name="z_neg")
            ge = ring.tile([P, K], F32, name="gate_e")
            gs = ring.tile([P, 1], F32, name="gate_s")
            gate[t] = ge
            inv_gates[t] = keep.tile([P, 1], F32, name="inv_gates%d" % t)

            def g1():
                nc.vector.tensor_reduce(out=neg[:], in_=z_ps[t][:], axis=AX.X, op=ALU.max, negate=True)
                nc.scalar.activation(ge[:], z_ps[t][:], ACT.Exp, bias=neg[:, 0:1], accum_out=gs[:, 0:1])

            def g2():
                nc.vector.reciprocal(inv_gates[t][:], gs[:])

            return [g1, None, None, g2]

        def mix_steps(job):
            t, c = divmod(job, CHUNKS)
            cols = slice(c * CHUNK, (c + 1) * CHUNK)
            if c == 0:
                mixed[t] = keep.tile([P, V], F32, name="mixed%d" % t)
            n = PE_TERMS.get(job, 0)
            acc = mixed[t][:, cols]

            def column(k):
                return weight[t][:, k, c : c + 1]

            diags = []
            for k in range(n):
                d = ring.tile([P, P], F32, name="diag", bufs=6)
                nc.gpsimd.tensor_scalar(d[:], ident[:], column(k), 0.0, ALU.mult, ALU.add)
                diags.append(d)

            def term(k):
                def run():
                    if k == 0:
                        banks[job] = ps_mix.tile([P, CHUNK], F32, name="mix_bank", tag="mix")
                    nc.tensor.matmul(
                        banks[job][:], lhsT=diags[k][:], rhs=expo[t * K + k][:, cols], start=(k == 0), stop=(k == n - 1)
                    )

                return run

            def scaled():
                nc.scalar.activation(acc, expo[t * K][:, cols], ACT.Copy, scale=column(0))

            def add(k):
                def run():
                    nc.vector.scalar_tensor_tensor(
                        out=acc,
                        in0=expo[t * K + k][:, cols],
                        scalar=column(k),
                        in1=(banks[job][:] if k == n else acc),
                        op0=ALU.mult,
                        op1=ALU.add,
                    )

                return run

            if n == 0:
                return [], [scaled] + [add(k) for k in range(1, K)]
            return [term(k) for k in range(n)], [add(k) for k in range(n, K)]

        banks = {}
        inv_gates = {}

        def log(t, lo, hi):
            nc.scalar.activation(mixed[t][:, lo:hi], mixed[t][:, lo:hi], ACT.Ln, bias=floor[:, 0:1], scale=inv_gates[t][:, 0:1])

        def finish(t, lo, hi):
            part = mixed[t][:, lo:hi]
            nc.vector.tensor_scalar(part, part, math.log(V) - LN_SHIFT * math.log(2.0), None, ALU.add)
            nc.sync.dma_start(out=out[t * P : (t + 1) * P, lo:hi], in_=part)

        W = PACK * D
        SPLIT = W // 4
        ALL = [0, 1, 2, 3]
        prep_h(0)
        pack_h(0)
        widen(0, nc.scalar.copy, 0, SPLIT)
        widen(0, nc.vector.tensor_copy, SPLIT, W)
        scale_w(0, ALL[3:], True)
        scale_w(0, ALL[:3], False)
        quant_w(0)
        widen(1, nc.scalar.copy, 0, W)
        first(0)
        scale_w(1, ALL, False)
        gain(0, nc.vector)
        quant_a(0)
        for c in range(CHUNKS):
            second(0, c)
        quant_w(1)
        first(1)
        gain(1, GAIN(nc))
        mixture_logit(0)
        widen(2, nc.scalar.copy, 0, W)
        prep_h(1)
        pack_h(1)

        small = []
        large = []
        terms = []
        fresh = []
        coming = ([], [])

        def one(queue):
            step = queue.pop(0) if queue else None
            if step:
                step()

        for i in range(UNITS):
            t, k = divmod(i, K)
            if k == 3:
                small += gate_steps(t)
            if k == 0 and t > 0:
                small += weight_steps(t - 1, 0, K)
            if i == UNITS - 1:
                small += weight_steps(t, 0, K - 1)
            job = i - K - LAG
            large += fresh
            fresh = coming[1]
            terms += coming[0]
            coming = mix_steps(job) if job >= 0 else ([], [])
            for c in range(CHUNKS):
                exps(i, c)
                one(small)
                if c == 0 and i <= 2:
                    quant_a(i + 1)
                if c == 2 and i >= 2:
                    quant_a(i + 2)
                if c == 1 and i == 0:
                    scale_w(2, ALL, False)
                    quant_w(2)
                if c == 1 and i == 1:
                    scale_w(3, ALL, True)
                    quant_w(3)
                second(i + 1, c)
                if c % 2:
                    one(large)
                    one(small)
                if c == 0 and i >= 2:
                    first(i + 3)
                    gain(i + 3, GAIN(nc))
                if c == 2:
                    mixture_logit(i + 1 if i < 2 else i + 2)
                if c >= 1:
                    one(terms)
            if i == 0:
                first(2)
                gain(2, GAIN(nc))
                widen(3, nc.scalar.copy, 0, W)
                prep_h(2)
                pack_h(2)
            if i == 1:
                first(3)
                gain(3, GAIN(nc))
                first(4)
                gain(4, GAIN(nc))
                prep_h(3)
                pack_h(3)
            if i == 2:
                mixture_logit(3)

        last = TILES - 1
        while small:
            one(small)
        jobs = [(terms + coming[0], coming[1])] + [mix_steps(job) for job in range(UNITS - K - LAG, UNITS - K)]
        large += fresh
        for mm, adds in jobs:
            for s in large:
                s()
            large = adds
            for s in mm:
                s()
        for s in large:
            s()
        fins = []
        for c in range(CHUNKS):
            mm, adds = mix_steps(last * K + c)
            for s in mm + adds[:-1]:
                s()
            fins.append(adds[-1])
        for t in range(last):
            log(t, 0, V)
        for s in weight_steps(last, K - 1, K):
            if s:
                s()
        for s in fins:
            s()
        for t in range(last):
            finish(t, 0, V)
        for c in range(CHUNKS):
            log(last, c * CHUNK, (c + 1) * CHUNK)
            finish(last, c * CHUNK, (c + 1) * CHUNK)
